import numpy as np
import ml_dtypes


def mxq(x, axis, fmt="e4m3"):
    dtype, down = {"e4m3": (ml_dtypes.float8_e4m3fn, 7), "e5m2": (ml_dtypes.float8_e5m2, 14)}[fmt]
    v = np.moveaxis(np.asarray(x, np.float32).astype(ml_dtypes.bfloat16).astype(np.float64), axis, -1)
    blocks = v.reshape(v.shape[:-1] + (-1, 32))
    amax = np.abs(blocks).max(-1, keepdims=True)
    byte = np.maximum(np.where(amax > 0, np.frexp(amax)[1] - 1 + 127, 0) - down, 1)
    scale = np.exp2(byte - 127.0)
    codes = (blocks / scale).astype(np.float32).astype(dtype).astype(np.float64)
    return np.moveaxis((codes * scale).reshape(v.shape), -1, axis)


WIDE = False


def mx_kscale(k):
    if not WIDE:
        return np.ones(k)
    levels = np.array([10, -10, 5, -5, 0])
    if k % 512:
        return np.exp2(np.random.permutation(np.resize(levels, k // 32))).repeat(32)
    a = np.empty((k // 512, 16))
    for p in range(k // 512):
        a[p, :8] = np.random.permutation(np.resize(levels, 8))
        for g in range(8):
            far = levels[np.abs(levels - a[p, g]) >= 10]
            a[p, g + 8] = far[np.random.randint(len(far))]
    return np.exp2(a.ravel()).repeat(32)


def f64(x):
    return np.asarray(x).astype(np.float64)


E2M1 = np.array([0.0, 0.5, 1.0, 1.5, 2.0, 3.0, 4.0, 6.0, -0.0, -0.5, -1.0, -1.5, -2.0, -3.0, -4.0, -6.0])


def pack_weight(w, fmt):
    k, n = w.shape
    w = f64(np.asarray(w, np.float32).astype(ml_dtypes.bfloat16)).reshape(k // 32, 32, n)
    amax = np.abs(w).max(1)
    if fmt == "e4m3":
        byte = np.frexp(amax)[1] - 1 + 127 - 7
    else:
        mant, ex = np.frexp(amax / 6.0)
        byte = np.where(mant > 0.5, ex, ex - 1) + 127
    byte = np.clip(np.where(amax > 0, byte, 1), 1, 254)
    scaled = (w * np.exp2(127.0 - byte)[:, None, :]).reshape(k, n).astype(np.float32)
    by_word = np.ascontiguousarray(scaled.reshape(k // 512, 128, 4, n).transpose(0, 1, 3, 2))
    if fmt == "e4m3":
        words = by_word.astype(ml_dtypes.float8_e4m3fn).view(np.uint8)
    else:
        c = by_word.astype(ml_dtypes.float4_e2m1fn).view(np.uint8) & 0xF
        words = (c[..., 0::2] | (c[..., 1::2] << 4)).reshape(k // 512, 128, 2 * n)
    return np.ascontiguousarray(words), np.ascontiguousarray(byte.astype(np.uint8).reshape(k // 512, 16, n))


def unpack_weight(words, scales, fmt):
    g, _, n = scales.shape
    words = np.ascontiguousarray(words).reshape(g, 128, n, -1)
    if fmt == "e4m3":
        vals = words.view(ml_dtypes.float8_e4m3fn).astype(np.float64)
    else:
        nib = np.empty((g, 128, n, 4), np.uint8)
        nib[..., 0::2] = words & 0xF
        nib[..., 1::2] = words >> 4
        vals = E2M1[nib]
    vals = vals * np.repeat(np.exp2(scales.astype(np.float64) - 127.0), 8, axis=1)[..., None]
    return vals.transpose(0, 1, 3, 2).reshape(g * 512, n)


def bf(x):
    return np.asarray(x, np.float32).astype(ml_dtypes.bfloat16)


def planes(Y):
    r, m = Y.shape
    b = f64(bf(Y)).reshape(r // 32, 32, m)
    amax = np.abs(b).max(1)
    byte = np.clip(np.where(amax > 0, np.frexp(amax)[1] - 1 + 127 - 7, 1), 1, 254)
    codes = (b * np.exp2(127.0 - byte)[:, None, :]).reshape(r, m).astype(np.float32).astype(ml_dtypes.float8_e4m3fn).view(np.uint8)
    words = codes.reshape(r // 512, 128, 4, m).transpose(0, 1, 3, 2)
    return np.ascontiguousarray(words), np.ascontiguousarray(byte.astype(np.uint8).reshape(r // 512, 16, m))


K, L, Q, I = 512, 1024, 512, 1024


def setup_inputs():
    n = np.random.standard_normal
    fk = mx_kscale(K)
    fl = mx_kscale(L)
    qap = pack_weight(n((K, Q)) * np.random.uniform(0.01, 0.1, (1, Q)) * fk[:, None], "e2m1")
    kap = pack_weight(n((K, I)) / fk[:, None], "e4m3")
    kbp = pack_weight(n((L, I)) / fl[:, None], "e2m1")
    return {
        "qa_words": qap[0],
        "qa_scales": qap[1],
        "ka_words": kap[0],
        "ka_scales": kap[1],
        "qb": (n((L, Q)) * np.random.uniform(0.005, 0.05, (1, Q)) * fl[:, None]).astype(np.float32),
        "kb_words": kbp[0],
        "kb_scales": kbp[1],
        "cw1": (np.random.uniform(0.5, 2.0, (1, I))).astype(np.float32),
    }


def reference(qa_words, qa_scales, ka_words, ka_scales, qb, kb_words, kb_scales, cw1):
    qau = unpack_weight(qa_words, qa_scales, "e2m1")
    kau = unpack_weight(ka_words, ka_scales, "e4m3")
    kbu = unpack_weight(kb_words, kb_scales, "e2m1")
    qbq = mxq(f64(qb), 0, "e4m3")
    a = qau.T @ kau + qbq.T @ kbu
    e = np.exp(0.7 * a / (np.mean(np.abs(a), axis=1, keepdims=True) + 0.1))
    y = 256.0 * e * f64(cw1) / np.sum(e, axis=1, keepdims=True)
    words, scales = planes(y)
    return y, words, scales

@@ -1,0 +1,302 @@
+from contextlib import ExitStack
+
+import concourse.mybir as mybir
+
+K, L, Q, I = 512, 1024, 512, 1024
+FLOPS = 2 * (K + L) * Q * I
+
+F32 = mybir.dt.float32
+BF16 = mybir.dt.bfloat16
+I32 = mybir.dt.int32
+U32 = mybir.dt.uint32
+U8 = mybir.dt.uint8
+FP8X4 = mybir.dt.float8_e4m3fn_x4
+FP4X4 = mybir.dt.float4_e2m1fn_x4
+ALU = mybir.AluOpType
+ACT = mybir.ActivationFunctionType
+AX = mybir.AxisListType
+
+P = 128
+PACK = 4
+BANK = 512
+HALVES = I // BANK
+M_VECTOR = 84
+CHUNK = 128
+SCALAR_CHUNKS = (0, 2, 4, 6, 7)
+
+
+def tile_mix_shares_by_row_scale_pl_kernel(
+    tc, qa_words, qa_scales, ka_words, ka_scales, qb, kb_words, kb_scales, cw1, out_0, out_1, out_2
+):
+    nc = tc.nc
+    with ExitStack() as ctx:
+        keep = ctx.enter_context(tc.tile_pool(name="keep", bufs=1))
+        psum = ctx.enter_context(tc.psum_pool(name="psum", bufs=1))
+        ctx.enter_context(tc.manual_schedule())
+
+        qb_raw = [keep.tile([P, PACK, Q], F32, name="qb_raw%d" % g) for g in range(2)]
+        qb_bf = [keep.tile([P, PACK, P, PACK], BF16, name="qb_bf%d" % g, align_bytes=64) for g in range(2)]
+        qb_codes = [keep.tile([P, Q], U32, name="qb_codes%d" % g, align_bytes=64) for g in range(2)]
+        qb_plane = [keep.tile([P, Q], U8, name="qb_plane%d" % g, align_bytes=64) for g in range(2)]
+        qa_raw = keep.tile([P, 2 * Q], U8, align_bytes=64)
+        qa_codes = keep.tile([P, 2 * Q], U8, align_bytes=64)
+        qa_plane_raw = keep.tile([P, Q], U8, align_bytes=64)
+        qa_plane = keep.tile([P, Q], U8, align_bytes=64)
+        ka_codes = [keep.tile([P, BANK], U32, name="ka_codes%d" % h, align_bytes=64) for h in range(HALVES)]
+        ka_plane = keep.tile([P, I], U8, align_bytes=64)
+        kb_codes = [keep.tile([P, 2 * I], U8, name="kb_codes%d" % g, align_bytes=64) for g in range(2)]
+        kb_plane = keep.tile([P, 2, I], U8, align_bytes=64)
+        cw = keep.tile([P, I], F32)
+        a = [keep.tile([P, I], F32, name="a%d" % t) for t in range(PACK)]
+        e = [keep.tile([P, I], F32, name="e%d" % t) for t in range(PACK)]
+        y = keep.tile([P, PACK, I], F32)
+        y_bf = keep.tile([P, I, PACK], BF16, align_bytes=64)
+        y_codes = keep.tile([P, I], U32, align_bytes=64)
+        y_plane = keep.tile([P, I], U8, align_bytes=64)
+        abs_sum = keep.tile([P, HALVES, PACK], F32)
+        exp_sum = keep.tile([P, PACK], F32)
+        run_max = keep.tile([P, HALVES, PACK], F32)
+        cw_raw = keep.tile([P, I], F32)
+        denom = keep.tile([P, PACK], F32)
+        sharp = keep.tile([P, PACK], F32)
+        shift = keep.tile([P, PACK], F32)
+        norm = keep.tile([P, PACK], F32)
+        acc = [[psum.tile([P, BANK], F32, name="acc%d_%d" % (t, h)) for h in range(HALVES)] for t in range(PACK)]
+
+        nc.vector.memset(kb_plane[:].rearrange("p z c -> p (z c)").bitcast(I32), 0)
+        nc.gpsimd.memset(qa_plane_raw[:].bitcast(I32), 0)
+        nc.vector.memset(ka_plane[:].bitcast(I32), 0)
+
+        def load_qb(g):
+            nc.sync.dma_start(out=qb_raw[g][:], in_=qb[g * 512 : (g + 1) * 512, :].rearrange("(p j) c -> p j c", j=PACK))
+
+        def load_ka(h):
+            words = ka_words[0].rearrange("p n t -> p (n t)")
+            nc.sync.dma_start(out=ka_codes[h][:].bitcast(I32), in_=words[:, 4 * BANK * h : 4 * BANK * (h + 1)].bitcast(I32))
+
+        def load_kb(g):
+            nc.sync.dma_start(out=kb_codes[g][:].bitcast(I32), in_=kb_words[g].bitcast(I32))
+
+        load_qb(0)
+        for u in range(4):
+            nc.sync.dma_start(
+                out=kb_plane[32 * u : 32 * u + 4, :, :].bitcast(I32),
+                in_=kb_scales[:, 4 * u : 4 * u + 4, :].rearrange("z r c -> r z c").bitcast(I32),
+            )
+        for u in range(4):
+            nc.gpsimd.dma_start(
+                out=qa_plane_raw[32 * u : 32 * u + 4, :].bitcast(I32), in_=qa_scales[0, 4 * u : 4 * u + 4, :].bitcast(I32)
+            )
+        load_kb(0)
+        nc.sync.dma_start(out=qa_raw[:].bitcast(I32), in_=qa_words[0].bitcast(I32))
+        load_qb(1)
+        for u in range(4):
+            nc.sync.dma_start(
+                out=ka_plane[32 * u : 32 * u + 4, :].bitcast(I32), in_=ka_scales[0, 4 * u : 4 * u + 4, :].bitcast(I32)
+            )
+        load_ka(0)
+        load_ka(1)
+        load_kb(1)
+        nc.sync.dma_start(out=cw_raw[:], in_=cw1[0].partition_broadcast(P))
+
+        def round_qb(g):
+            src = qb_raw[g][:].rearrange("p j (m t) -> p m t j", t=PACK)
+            dst = qb_bf[g][:].rearrange("p t m j -> p m t j")
+            nc.vector.tensor_copy(out=dst[:, :M_VECTOR], in_=src[:, :M_VECTOR])
+            nc.scalar.activation(out=dst[:, M_VECTOR:], in_=src[:, M_VECTOR:], func=ACT.Copy)
+
+        def quantize_qb(g, t0, t1):
+            nc.vector.quantize_mx(
+                out=qb_codes[g][:, t0 * P : t1 * P].bitcast(FP8X4),
+                scales=qb_plane[g][:, t0 * P : t1 * P],
+                in_=qb_bf[g][:, t0:t1].rearrange("p t m j -> p (t m j)"),
+            )
+
+        def product_b(g, t, h, start, stop):
+            nc.tensor.matmul_mx(
+                out=acc[t][h][:],
+                lhsT=qb_codes[g][:, t * P : (t + 1) * P].bitcast(FP8X4),
+                lhsT_scale=qb_plane[g][:, t * P : (t + 1) * P],
+                rhs=kb_codes[g][:, 2 * BANK * h : 2 * BANK * (h + 1)].bitcast(FP4X4),
+                rhs_scale=kb_plane[:, g, BANK * h : BANK * (h + 1)],
+                start=start,
+                stop=stop,
+            )
+
+        def product_a(t, h, stop):
+            nc.tensor.matmul_mx(
+                out=acc[t][h][:],
+                lhsT=qa_codes[:, 2 * P * t : 2 * P * (t + 1)].bitcast(FP4X4),
+                lhsT_scale=qa_plane[:, t * P : (t + 1) * P],
+                rhs=ka_codes[h][:].bitcast(FP8X4),
+                rhs_scale=ka_plane[:, BANK * h : BANK * (h + 1)],
+                start=False,
+                stop=stop,
+            )
+
+        round_qb(0)
+        quantize_qb(0, 0, 2)
+        quantize_qb(0, 2, 4)
+        for t in range(PACK):
+            for h in range(HALVES):
+                product_b(0, t, h, True, False)
+        nc.vector.tensor_copy(
+            out=qa_codes[:].rearrange("p (t m b) -> p t m b", t=PACK, b=2),
+            in_=qa_raw[:].rearrange("p (m t b) -> p t m b", t=PACK, b=2),
+        )
+        round_qb(1)
+        nc.vector.tensor_copy(
+            out=qa_plane[:].rearrange("p (t m) -> p t m", t=PACK),
+            in_=qa_plane_raw[:].rearrange("p (m t) -> p t m", t=PACK),
+        )
+        for t in range(PACK):
+            quantize_qb(1, t, t + 1)
+        for t in range(PACK):
+            for h in range(HALVES):
+                product_a(t, h, False)
+            for h in range(HALVES):
+                product_b(1, t, h, False, True)
+
+        def half(h):
+            return slice(h * BANK, (h + 1) * BANK)
+
+        def sum_abs(t, h):
+            nc.scalar.activation(
+                out=e[t][:, half(h)], in_=acc[t][h][:], func=ACT.Abs, scale=1.0 / (0.7 * I), accum_out=abs_sum[:, h, t : t + 1]
+            )
+
+        def find_max(t, h):
+            nc.vector.tensor_scalar(
+                out=a[t][:, half(h)],
+                in0=acc[t][h][:],
+                scalar1=1.0,
+                scalar2=None if h == 0 else run_max[:, 0, t : t + 1],
+                op0=ALU.mult,
+                op1=ALU.max,
+                accum_out=run_max[:, h, t : t + 1],
+            )
+
+        def make_denom(t0):
+            two = slice(t0, t0 + 2)
+            nc.vector.scalar_tensor_tensor(
+                out=denom[:, two], in0=abs_sum[:, 0, two], scalar=0.1 / 0.7, in1=abs_sum[:, 1, two], op0=ALU.add, op1=ALU.add
+            )
+
+        def make_sharp(t0):
+            two = slice(t0, t0 + 2)
+            nc.vector.reciprocal(out=sharp[:, two], in_=denom[:, two])
+
+        def make_shift(t0):
+            two = slice(t0, t0 + 2)
+            nc.vector.scalar_tensor_tensor(
+                out=shift[:, two], in0=run_max[:, 1, two], scalar=-1.0, in1=sharp[:, two], op0=ALU.mult, op1=ALU.mult
+            )
+
+        def exponentiate(t):
+            nc.scalar.activation(
+                out=e[t][:],
+                in_=a[t][:],
+                func=ACT.Exp,
+                scale=sharp[:, t : t + 1],
+                bias=shift[:, t : t + 1],
+                accum_out=exp_sum[:, t : t + 1],
+            )
+
+        def make_norm(t):
+            nc.vector.reciprocal(out=norm[:, t : t + 1], in_=exp_sum[:, t : t + 1])
+
+        def weigh(t, c0, c1):
+            nc.vector.scalar_tensor_tensor(
+                out=y[:, t, c0:c1], in0=e[t][:, c0:c1], scalar=norm[:, t : t + 1], in1=cw[:, c0:c1], op0=ALU.mult, op1=ALU.mult
+            )
+
+        out_rows = out_0.rearrange("(p t) c -> p t c", t=PACK)
+
+        def store_y(t, c0, c1):
+            nc.sync.dma_start(out=out_rows[:, t, c0:c1], in_=y[:, t, c0:c1])
+
+        def round_y(n):
+            cols = slice(n * CHUNK, (n + 1) * CHUNK)
+            src = y[:, :, cols].rearrange("p t (c i) -> p c t i", i=4)
+            dst = y_bf[:, cols, :].rearrange("p (c i) t -> p c t i", i=4)
+            if n in SCALAR_CHUNKS:
+                nc.scalar.activation(out=dst, in_=src, func=ACT.Copy)
+            else:
+                nc.vector.tensor_copy(out=dst, in_=src)
+
+        def quantize_y(n):
+            cols = slice(n * CHUNK, (n + 1) * CHUNK)
+            nc.vector.quantize_mx(
+                out=y_codes[:, cols].bitcast(FP8X4), scales=y_plane[:, cols], in_=y_bf[:, cols, :].rearrange("p c t -> p (c t)")
+            )
+
+        code_rows = out_1[0].rearrange("p n t -> p (n t)").bitcast(I32)
+
+        def store_codes(c0, c1):
+            nc.sync.dma_start(out=code_rows[:, c0:c1], in_=y_codes[:, c0:c1].bitcast(I32))
+
+        nc.gpsimd.tensor_scalar(out=cw[:], in0=cw_raw[:], scalar1=256.0, scalar2=0.0, op0=ALU.mult, op1=ALU.add)
+        for t in (0, 1):
+            for h in range(HALVES):
+                sum_abs(t, h)
+                if (t, h) == (1, 1):
+                    make_denom(0)
+                find_max(t, h)
+        make_sharp(0)
+        make_shift(0)
+        sum_abs(2, 0)
+        sum_abs(2, 1)
+        find_max(3, 0)
+        exponentiate(0)
+        find_max(3, 1)
+        make_norm(0)
+        sum_abs(3, 0)
+        sum_abs(3, 1)
+        find_max(2, 0)
+        find_max(2, 1)
+        exponentiate(1)
+        make_denom(2)
+        weigh(0, 0, BANK)
+        make_sharp(2)
+        make_shift(2)
+        weigh(0, BANK, I)
+        store_y(0, 0, I)
+        exponentiate(2)
+        make_norm(1)
+        weigh(1, 0, I)
+        store_y(1, 0, I)
+        exponentiate(3)
+        make_norm(2)
+        weigh(2, 0, BANK)
+        make_norm(3)
+        weigh(2, BANK, I)
+        store_y(2, 0, I)
+
+        weigh(3, 0, 256)
+        round_y(0)
+        weigh(3, 256, 512)
+        store_y(3, 0, BANK)
+        round_y(2)
+        round_y(1)
+        weigh(3, 512, 768)
+        round_y(4)
+        quantize_y(0)
+        weigh(3, 768, 1024)
+        store_y(3, BANK, I)
+        round_y(6)
+        round_y(7)
+        quantize_y(1)
+        round_y(3)
+        quantize_y(2)
+        round_y(5)
+        quantize_y(3)
+        store_codes(0, BANK)
+        quantize_y(4)
+        quantize_y(5)
+        quantize_y(6)
+        store_codes(BANK, 7 * CHUNK)
+        quantize_y(7)
+        store_codes(7 * CHUNK, I)
+        for u in range(4):
+            queue = nc.scalar if u % 2 == 0 else nc.sync
+            queue.dma_start(out=out_2[0, 4 * u : 4 * u + 4, :].bitcast(I32), in_=y_plane[32 * u : 32 * u + 4, :].bitcast(I32))

@@ -1,6 +1,7 @@
 from contextlib import ExitStack
 
 import concourse.mybir as mybir
+from concourse.masks import make_identity
 
 K, L, Q, I = 512, 1024, 512, 1024
 FLOPS = 2 * (K + L) * Q * I
@@ -21,8 +22,6 @@ PACK = 4
 BANK = 512
 HALVES = I // BANK
 M_VECTOR = 84
-CHUNK = 128
-SCALAR_CHUNKS = (0, 2, 4, 6, 7)
 
 
 def tile_mix_shares_by_row_scale_pl_kernel(
@@ -53,19 +52,28 @@ def tile_mix_shares_by_row_scale_pl_kernel(
         y_bf = keep.tile([P, I, PACK], BF16, align_bytes=64)
         y_codes = keep.tile([P, I], U32, align_bytes=64)
         y_plane = keep.tile([P, I], U8, align_bytes=64)
-        abs_sum = keep.tile([P, HALVES, PACK], F32)
+        sums = keep.tile([P, PACK, 4], F32)
+        prods = keep.tile([P, PACK, 4], F32)
+        ones = keep.tile([P, PACK], F32)
+        first_max = keep.tile([P, PACK], F32)
         exp_sum = keep.tile([P, PACK], F32)
-        run_max = keep.tile([P, HALVES, PACK], F32)
-        cw_raw = keep.tile([P, I], F32)
         denom = keep.tile([P, PACK], F32)
-        sharp = keep.tile([P, PACK], F32)
         shift = keep.tile([P, PACK], F32)
         norm = keep.tile([P, PACK], F32)
+        cw_rows = keep.tile([P, HALVES, 8], F32)
+        cw_cols = keep.tile([P, HALVES, 4], F32)
+        ident = keep.tile([P, P], F32)
+        u0 = keep.tile([P, I], F32)
+        u1 = keep.tile([P, BANK], F32)
         acc = [[psum.tile([P, BANK], F32, name="acc%d_%d" % (t, h)) for h in range(HALVES)] for t in range(PACK)]
 
         nc.vector.memset(kb_plane[:].rearrange("p z c -> p (z c)").bitcast(I32), 0)
+        nc.vector.memset(ident[:], 0.0)
         nc.gpsimd.memset(qa_plane_raw[:].bitcast(I32), 0)
         nc.vector.memset(ka_plane[:].bitcast(I32), 0)
+        nc.vector.memset(ones[:], 1.0)
+        nc.vector.memset(prods[:, :, 2], -1.0)
+        nc.vector.tensor_scalar(out=sums[:, :, 2], in0=ones[:], scalar1=0.1 / 0.7, scalar2=None, op0=ALU.mult)
 
         def load_qb(g):
             nc.sync.dma_start(out=qb_raw[g][:], in_=qb[g * 512 : (g + 1) * 512, :].rearrange("(p j) c -> p j c", j=PACK))
@@ -77,6 +85,7 @@ def tile_mix_shares_by_row_scale_pl_kernel(
         def load_kb(g):
             nc.sync.dma_start(out=kb_codes[g][:].bitcast(I32), in_=kb_words[g].bitcast(I32))
 
+        nc.sync.dma_start(out=cw_rows[:, :, :4], in_=cw1[0].rearrange("(h p c) -> p h c", h=HALVES, c=4))
         load_qb(0)
         for u in range(4):
             nc.sync.dma_start(
@@ -87,6 +96,8 @@ def tile_mix_shares_by_row_scale_pl_kernel(
             nc.gpsimd.dma_start(
                 out=qa_plane_raw[32 * u : 32 * u + 4, :].bitcast(I32), in_=qa_scales[0, 4 * u : 4 * u + 4, :].bitcast(I32)
             )
+            if u == 0:
+                make_identity(nc, ident[:], nomemset=True)
         load_kb(0)
         nc.sync.dma_start(out=qa_raw[:].bitcast(I32), in_=qa_words[0].bitcast(I32))
         load_qb(1)
@@ -94,10 +105,9 @@ def tile_mix_shares_by_row_scale_pl_kernel(
             nc.sync.dma_start(
                 out=ka_plane[32 * u : 32 * u + 4, :].bitcast(I32), in_=ka_scales[0, 4 * u : 4 * u + 4, :].bitcast(I32)
             )
+        load_kb(1)
         load_ka(0)
         load_ka(1)
-        load_kb(1)
-        nc.sync.dma_start(out=cw_raw[:], in_=cw1[0].partition_broadcast(P))
 
         def round_qb(g):
             src = qb_raw[g][:].rearrange("p j (m t) -> p m t j", t=PACK)
@@ -134,10 +144,23 @@ def tile_mix_shares_by_row_scale_pl_kernel(
                 stop=stop,
             )
 
+        def spread_cw(banks):
+            for h in range(HALVES):
+                for c in range(4):
+                    nc.tensor.transpose(
+                        banks[h][:].rearrange("p (n c) -> p c n", c=4)[:, c],
+                        cw_cols[:, h, c : c + 1].to_broadcast([P, P]),
+                        ident[:],
+                    )
+
+        nc.vector.tensor_scalar(out=cw_cols[:], in0=cw_rows[:, :, :4], scalar1=256.0, scalar2=None, op0=ALU.mult)
+        spread_cw(acc[3])
         round_qb(0)
-        quantize_qb(0, 0, 2)
-        quantize_qb(0, 2, 4)
         for t in range(PACK):
+            quantize_qb(0, t, t + 1)
+        for h in range(HALVES):
+            nc.scalar.copy(out=cw[:, h * BANK : (h + 1) * BANK], in_=acc[3][h][:])
+        for t in range(PACK - 1):
             for h in range(HALVES):
                 product_b(0, t, h, True, False)
         nc.vector.tensor_copy(
@@ -145,24 +168,28 @@ def tile_mix_shares_by_row_scale_pl_kernel(
             in_=qa_raw[:].rearrange("p (m t b) -> p t m b", t=PACK, b=2),
         )
         round_qb(1)
+        quantize_qb(1, 0, 1)
         nc.vector.tensor_copy(
             out=qa_plane[:].rearrange("p (t m) -> p t m", t=PACK),
             in_=qa_plane_raw[:].rearrange("p (m t) -> p t m", t=PACK),
         )
-        for t in range(PACK):
+        for t in range(1, PACK):
             quantize_qb(1, t, t + 1)
         for t in range(PACK):
+            if t == PACK - 1:
+                for h in range(HALVES):
+                    product_b(0, t, h, True, False)
             for h in range(HALVES):
-                product_a(t, h, False)
+                product_b(1, t, h, False, False)
             for h in range(HALVES):
-                product_b(1, t, h, False, True)
+                product_a(t, h, True)
 
         def half(h):
             return slice(h * BANK, (h + 1) * BANK)
 
         def sum_abs(t, h):
             nc.scalar.activation(
-                out=e[t][:, half(h)], in_=acc[t][h][:], func=ACT.Abs, scale=1.0 / (0.7 * I), accum_out=abs_sum[:, h, t : t + 1]
+                out=e[t][:, half(h)], in_=acc[t][h][:], func=ACT.Abs, scale=1.0 / (0.7 * I), accum_out=sums[:, t, h : h + 1]
             )
 
         def find_max(t, h):
@@ -170,34 +197,27 @@ def tile_mix_shares_by_row_scale_pl_kernel(
                 out=a[t][:, half(h)],
                 in0=acc[t][h][:],
                 scalar1=1.0,
-                scalar2=None if h == 0 else run_max[:, 0, t : t + 1],
+                scalar2=None if h == 0 else first_max[:, t : t + 1],
                 op0=ALU.mult,
                 op1=ALU.max,
-                accum_out=run_max[:, h, t : t + 1],
+                accum_out=first_max[:, t : t + 1] if h == 0 else prods[:, t, 0:1],
             )
 
-        def make_denom(t0):
-            two = slice(t0, t0 + 2)
-            nc.vector.scalar_tensor_tensor(
-                out=denom[:, two], in0=abs_sum[:, 0, two], scalar=0.1 / 0.7, in1=abs_sum[:, 1, two], op0=ALU.add, op1=ALU.add
-            )
+        def make_denom(t):
+            nc.vector.tensor_reduce(out=denom[:, t : t + 1], in_=sums[:, t, 0:3], axis=AX.X, op=ALU.add)
 
-        def make_sharp(t0):
-            two = slice(t0, t0 + 2)
-            nc.vector.reciprocal(out=sharp[:, two], in_=denom[:, two])
+        def make_sharp(t):
+            nc.vector.reciprocal(out=prods[:, t, 1:2], in_=denom[:, t : t + 1])
 
-        def make_shift(t0):
-            two = slice(t0, t0 + 2)
-            nc.vector.scalar_tensor_tensor(
-                out=shift[:, two], in0=run_max[:, 1, two], scalar=-1.0, in1=sharp[:, two], op0=ALU.mult, op1=ALU.mult
-            )
+        def make_shift(t):
+            nc.vector.tensor_reduce(out=shift[:, t : t + 1], in_=prods[:, t, 0:3], axis=AX.X, op=ALU.mult)
 
         def exponentiate(t):
             nc.scalar.activation(
                 out=e[t][:],
                 in_=a[t][:],
                 func=ACT.Exp,
-                scale=sharp[:, t : t + 1],
+                scale=prods[:, t, 1:2],
                 bias=shift[:, t : t + 1],
                 accum_out=exp_sum[:, t : t + 1],
             )
@@ -206,28 +226,38 @@ def tile_mix_shares_by_row_scale_pl_kernel(
             nc.vector.reciprocal(out=norm[:, t : t + 1], in_=exp_sum[:, t : t + 1])
 
         def weigh(t, c0, c1):
+            h = c0 // BANK
             nc.vector.scalar_tensor_tensor(
-                out=y[:, t, c0:c1], in0=e[t][:, c0:c1], scalar=norm[:, t : t + 1], in1=cw[:, c0:c1], op0=ALU.mult, op1=ALU.mult
+                out=y[:, t, c0:c1],
+                in0=e[t][:, c0:c1],
+                scalar=norm[:, t : t + 1],
+                in1=acc[0][h][:, c0 - h * BANK : c1 - h * BANK],
+                op0=ALU.mult,
+                op1=ALU.mult,
             )
+
+        def weigh_first(u, t, c0):
+            nc.gpsimd.tensor_tensor(out=u[:], in0=e[t][:, c0:], in1=cw[:, c0:], op=ALU.mult)
+
+        def weigh_second(u, t, c0):
+            nc.gpsimd.tensor_scalar(out=y[:, t, c0:], in0=u[:], scalar1=norm[:, t : t + 1], scalar2=0.0, op0=ALU.mult, op1=ALU.add)
 
         out_rows = out_0.rearrange("(p t) c -> p t c", t=PACK)
 
         def store_y(t, c0, c1):
             nc.sync.dma_start(out=out_rows[:, t, c0:c1], in_=y[:, t, c0:c1])
 
-        def round_y(n):
-            cols = slice(n * CHUNK, (n + 1) * CHUNK)
-            src = y[:, :, cols].rearrange("p t (c i) -> p c t i", i=4)
-            dst = y_bf[:, cols, :].rearrange("p (c i) t -> p c t i", i=4)
-            if n in SCALAR_CHUNKS:
+        def round_y(c0, c1, on_scalar):
+            src = y[:, :, c0:c1].rearrange("p t (c i) -> p c t i", i=4)
+            dst = y_bf[:, c0:c1, :].rearrange("p (c i) t -> p c t i", i=4)
+            if on_scalar:
                 nc.scalar.activation(out=dst, in_=src, func=ACT.Copy)
             else:
                 nc.vector.tensor_copy(out=dst, in_=src)
 
-        def quantize_y(n):
-            cols = slice(n * CHUNK, (n + 1) * CHUNK)
+        def quantize_y(c0, c1):
             nc.vector.quantize_mx(
-                out=y_codes[:, cols].bitcast(FP8X4), scales=y_plane[:, cols], in_=y_bf[:, cols, :].rearrange("p c t -> p (c t)")
+                out=y_codes[:, c0:c1].bitcast(FP8X4), scales=y_plane[:, c0:c1], in_=y_bf[:, c0:c1, :].rearrange("p c t -> p (c t)")
             )
 
         code_rows = out_1[0].rearrange("p n t -> p (n t)").bitcast(I32)
@@ -235,68 +265,71 @@ def tile_mix_shares_by_row_scale_pl_kernel(
         def store_codes(c0, c1):
             nc.sync.dma_start(out=code_rows[:, c0:c1], in_=y_codes[:, c0:c1].bitcast(I32))
 
-        nc.gpsimd.tensor_scalar(out=cw[:], in0=cw_raw[:], scalar1=256.0, scalar2=0.0, op0=ALU.mult, op1=ALU.add)
-        for t in (0, 1):
-            for h in range(HALVES):
-                sum_abs(t, h)
-                if (t, h) == (1, 1):
-                    make_denom(0)
-                find_max(t, h)
+        sum_abs(0, 0)
+        find_max(0, 0)
+        sum_abs(0, 1)
+        make_denom(0)
+        find_max(0, 1)
         make_sharp(0)
-        make_shift(0)
+        spread_cw(acc[0])
+        sum_abs(1, 0)
+        sum_abs(1, 1)
         sum_abs(2, 0)
-        sum_abs(2, 1)
-        find_max(3, 0)
+        find_max(1, 0)
+        make_shift(0)
         exponentiate(0)
-        find_max(3, 1)
-        make_norm(0)
+        make_denom(1)
+        find_max(1, 1)
+        make_sharp(1)
+        weigh_first(u0, 0, 0)
+        sum_abs(2, 1)
         sum_abs(3, 0)
         sum_abs(3, 1)
         find_max(2, 0)
-        find_max(2, 1)
+        make_shift(1)
         exponentiate(1)
-        make_denom(2)
-        weigh(0, 0, BANK)
-        make_sharp(2)
-        make_shift(2)
-        weigh(0, BANK, I)
+        make_norm(0)
+        weigh_second(u0, 0, 0)
         store_y(0, 0, I)
+        make_denom(2)
+        find_max(2, 1)
+        make_sharp(2)
+        find_max(3, 0)
+        make_shift(2)
         exponentiate(2)
+        make_denom(3)
+        find_max(3, 1)
+        make_sharp(3)
         make_norm(1)
-        weigh(1, 0, I)
-        store_y(1, 0, I)
+        weigh_first(u1, 1, BANK)
+        weigh_second(u1, 1, BANK)
+        make_shift(3)
         exponentiate(3)
+        weigh(1, 0, BANK)
         make_norm(2)
         weigh(2, 0, BANK)
-        make_norm(3)
         weigh(2, BANK, I)
         store_y(2, 0, I)
+        store_y(1, 0, I)
+        make_norm(3)
 
         weigh(3, 0, 256)
-        round_y(0)
+        round_y(0, 256, True)
         weigh(3, 256, 512)
         store_y(3, 0, BANK)
-        round_y(2)
-        round_y(1)
-        weigh(3, 512, 768)
-        round_y(4)
-        quantize_y(0)
-        weigh(3, 768, 1024)
+        weigh(3, 512, 1024)
         store_y(3, BANK, I)
-        round_y(6)
-        round_y(7)
-        quantize_y(1)
-        round_y(3)
-        quantize_y(2)
-        round_y(5)
-        quantize_y(3)
+        round_y(256, 512, False)
+        round_y(512, 768, True)
+        quantize_y(0, 256)
+        round_y(832, 1024, False)
+        quantize_y(256, 512)
         store_codes(0, BANK)
-        quantize_y(4)
-        quantize_y(5)
-        quantize_y(6)
-        store_codes(BANK, 7 * CHUNK)
-        quantize_y(7)
-        store_codes(7 * CHUNK, I)
+        round_y(768, 832, True)
+        quantize_y(512, 768)
+        store_codes(BANK, 768)
+        quantize_y(768, 1024)
+        store_codes(768, I)
         for u in range(4):
             queue = nc.scalar if u % 2 == 0 else nc.sync
             queue.dma_start(out=out_2[0, 4 * u : 4 * u + 4, :].bitcast(I32), in_=y_plane[32 * u : 32 * u + 4, :].bitcast(I32))

@@ -69,6 +69,8 @@ def tile_mix_shares_by_row_scale_pl_kernel(
 
         nc.vector.memset(kb_plane[:].rearrange("p z c -> p (z c)").bitcast(I32), 0)
         nc.vector.memset(ident[:], 0.0)
+        nc.gpsimd.dma_start(out=cw_rows[:, :, :4], in_=cw1[0].rearrange("(h p c) -> p h c", h=HALVES, c=4))
+        make_identity(nc, ident[:], nomemset=True)
         nc.gpsimd.memset(qa_plane_raw[:].bitcast(I32), 0)
         nc.vector.memset(ka_plane[:].bitcast(I32), 0)
         nc.vector.memset(ones[:], 1.0)
@@ -85,25 +87,22 @@ def tile_mix_shares_by_row_scale_pl_kernel(
         def load_kb(g):
             nc.sync.dma_start(out=kb_codes[g][:].bitcast(I32), in_=kb_words[g].bitcast(I32))
 
-        nc.sync.dma_start(out=cw_rows[:, :, :4], in_=cw1[0].rearrange("(h p c) -> p h c", h=HALVES, c=4))
         load_qb(0)
         for u in range(4):
             nc.sync.dma_start(
-                out=kb_plane[32 * u : 32 * u + 4, :, :].bitcast(I32),
-                in_=kb_scales[:, 4 * u : 4 * u + 4, :].rearrange("z r c -> r z c").bitcast(I32),
+                out=kb_plane[u:P:32, :, :].bitcast(I32),
+                in_=kb_scales[:, u:16:4, :].rearrange("z r c -> r z c").bitcast(I32),
             )
         for u in range(4):
             nc.gpsimd.dma_start(
-                out=qa_plane_raw[32 * u : 32 * u + 4, :].bitcast(I32), in_=qa_scales[0, 4 * u : 4 * u + 4, :].bitcast(I32)
+                out=qa_plane_raw[u:P:32, :].bitcast(I32), in_=qa_scales[0, u:16:4, :].bitcast(I32)
             )
-            if u == 0:
-                make_identity(nc, ident[:], nomemset=True)
         load_kb(0)
         nc.sync.dma_start(out=qa_raw[:].bitcast(I32), in_=qa_words[0].bitcast(I32))
         load_qb(1)
         for u in range(4):
             nc.sync.dma_start(
-                out=ka_plane[32 * u : 32 * u + 4, :].bitcast(I32), in_=ka_scales[0, 4 * u : 4 * u + 4, :].bitcast(I32)
+                out=ka_plane[u:P:32, :].bitcast(I32), in_=ka_scales[0, u:16:4, :].bitcast(I32)
             )
         load_kb(1)
         load_ka(0)
@@ -144,29 +143,29 @@ def tile_mix_shares_by_row_scale_pl_kernel(
                 stop=stop,
             )
 
-        def spread_cw(banks):
+        def spread_cw(banks, src):
             for h in range(HALVES):
                 for c in range(4):
                     nc.tensor.transpose(
                         banks[h][:].rearrange("p (n c) -> p c n", c=4)[:, c],
-                        cw_cols[:, h, c : c + 1].to_broadcast([P, P]),
+                        src[:, h, c : c + 1].to_broadcast([P, P]),
                         ident[:],
                     )
 
-        nc.vector.tensor_scalar(out=cw_cols[:], in0=cw_rows[:, :, :4], scalar1=256.0, scalar2=None, op0=ALU.mult)
-        spread_cw(acc[3])
+        spread_cw(acc[3], cw_rows)
         round_qb(0)
         for t in range(PACK):
             quantize_qb(0, t, t + 1)
         for h in range(HALVES):
-            nc.scalar.copy(out=cw[:, h * BANK : (h + 1) * BANK], in_=acc[3][h][:])
-        for t in range(PACK - 1):
+            nc.scalar.activation(out=cw[:, h * BANK : (h + 1) * BANK], in_=acc[3][h][:], func=ACT.Copy, scale=256.0)
+        for t in range(PACK):
             for h in range(HALVES):
                 product_b(0, t, h, True, False)
         nc.vector.tensor_copy(
             out=qa_codes[:].rearrange("p (t m b) -> p t m b", t=PACK, b=2),
             in_=qa_raw[:].rearrange("p (m t b) -> p t m b", t=PACK, b=2),
         )
+        nc.vector.tensor_scalar(out=cw_cols[:], in0=cw_rows[:, :, :4], scalar1=256.0, scalar2=None, op0=ALU.mult)
         round_qb(1)
         quantize_qb(1, 0, 1)
         nc.vector.tensor_copy(
@@ -176,9 +175,6 @@ def tile_mix_shares_by_row_scale_pl_kernel(
         for t in range(1, PACK):
             quantize_qb(1, t, t + 1)
         for t in range(PACK):
-            if t == PACK - 1:
-                for h in range(HALVES):
-                    product_b(0, t, h, True, False)
             for h in range(HALVES):
                 product_b(1, t, h, False, False)
             for h in range(HALVES):
@@ -271,7 +267,7 @@ def tile_mix_shares_by_row_scale_pl_kernel(
         make_denom(0)
         find_max(0, 1)
         make_sharp(0)
-        spread_cw(acc[0])
+        spread_cw(acc[0], cw_cols)
         sum_abs(1, 0)
         sum_abs(1, 1)
         sum_abs(2, 0)
@@ -332,4 +328,4 @@ def tile_mix_shares_by_row_scale_pl_kernel(
         store_codes(768, I)
         for u in range(4):
             queue = nc.scalar if u % 2 == 0 else nc.sync
-            queue.dma_start(out=out_2[0, 4 * u : 4 * u + 4, :].bitcast(I32), in_=y_plane[32 * u : 32 * u + 4, :].bitcast(I32))
+            queue.dma_start(out=out_2[0, u:16:4, :].bitcast(I32), in_=y_plane[u:P:32, :].bitcast(I32))

@@ -19,9 +19,18 @@ AX = mybir.AxisListType
 
 P = 128
 PACK = 4
+K_PASS = P * PACK
+B_PASSES = L // K_PASS
 BANK = 512
 HALVES = I // BANK
-M_VECTOR = 84
+QUADRANT = 32
+SCALE_ROWS = 16
+QUARTER = I // 4
+SHARPNESS = 0.7
+FLOOR = 0.1
+GAIN = 256.0
+QB_GROUPS_VECTOR = 84
+LAST_COLS_SCALAR = 64
 
 
 def tile_mix_shares_by_row_scale_pl_kernel(
@@ -33,299 +42,321 @@ def tile_mix_shares_by_row_scale_pl_kernel(
         psum = ctx.enter_context(tc.psum_pool(name="psum", bufs=1))
         ctx.enter_context(tc.manual_schedule())
 
-        qb_raw = [keep.tile([P, PACK, Q], F32, name="qb_raw%d" % g) for g in range(2)]
-        qb_bf = [keep.tile([P, PACK, P, PACK], BF16, name="qb_bf%d" % g, align_bytes=64) for g in range(2)]
-        qb_codes = [keep.tile([P, Q], U32, name="qb_codes%d" % g, align_bytes=64) for g in range(2)]
-        qb_plane = [keep.tile([P, Q], U8, name="qb_plane%d" % g, align_bytes=64) for g in range(2)]
+        qb_raw = [keep.tile([P, PACK, Q], F32, name="qb_raw%d" % g) for g in range(B_PASSES)]
+        qb_bf = [keep.tile([P, PACK, P, PACK], BF16, name="qb_bf%d" % g, align_bytes=64) for g in range(B_PASSES)]
+        qb_codes = [keep.tile([P, Q], U32, name="qb_codes%d" % g, align_bytes=64) for g in range(B_PASSES)]
+        qb_plane = [keep.tile([P, Q], U8, name="qb_plane%d" % g, align_bytes=64) for g in range(B_PASSES)]
         qa_raw = keep.tile([P, 2 * Q], U8, align_bytes=64)
         qa_codes = keep.tile([P, 2 * Q], U8, align_bytes=64)
         qa_plane_raw = keep.tile([P, Q], U8, align_bytes=64)
         qa_plane = keep.tile([P, Q], U8, align_bytes=64)
         ka_codes = [keep.tile([P, BANK], U32, name="ka_codes%d" % h, align_bytes=64) for h in range(HALVES)]
         ka_plane = keep.tile([P, I], U8, align_bytes=64)
-        kb_codes = [keep.tile([P, 2 * I], U8, name="kb_codes%d" % g, align_bytes=64) for g in range(2)]
-        kb_plane = keep.tile([P, 2, I], U8, align_bytes=64)
+        kb_codes = [keep.tile([P, 2 * I], U8, name="kb_codes%d" % g, align_bytes=64) for g in range(B_PASSES)]
+        kb_plane = keep.tile([P, B_PASSES, I], U8, align_bytes=64)
         cw = keep.tile([P, I], F32)
-        a = [keep.tile([P, I], F32, name="a%d" % t) for t in range(PACK)]
+        scores = [keep.tile([P, I], F32, name="scores%d" % t) for t in range(PACK)]
         e = [keep.tile([P, I], F32, name="e%d" % t) for t in range(PACK)]
-        y = keep.tile([P, PACK, I], F32)
+        y = keep.tile([P, HALVES, PACK, BANK], F32)
         y_bf = keep.tile([P, I, PACK], BF16, align_bytes=64)
         y_codes = keep.tile([P, I], U32, align_bytes=64)
         y_plane = keep.tile([P, I], U8, align_bytes=64)
-        sums = keep.tile([P, PACK, 4], F32)
-        prods = keep.tile([P, PACK, 4], F32)
+        terms = keep.tile([P, PACK, 4], F32)
+        factors = keep.tile([P, PACK, 4], F32)
         ones = keep.tile([P, PACK], F32)
         first_max = keep.tile([P, PACK], F32)
         exp_sum = keep.tile([P, PACK], F32)
-        denom = keep.tile([P, PACK], F32)
+        divisor = keep.tile([P, PACK], F32)
         shift = keep.tile([P, PACK], F32)
         norm = keep.tile([P, PACK], F32)
         cw_rows = keep.tile([P, HALVES, 8], F32)
-        cw_cols = keep.tile([P, HALVES, 4], F32)
+        cw_gained = keep.tile([P, HALVES, PACK], F32)
         ident = keep.tile([P, P], F32)
-        u0 = keep.tile([P, I], F32)
-        u1 = keep.tile([P, BANK], F32)
+        e_cw0 = keep.tile([P, I], F32)
+        e_cw2 = keep.tile([P, BANK], F32)
         acc = [[psum.tile([P, BANK], F32, name="acc%d_%d" % (t, h)) for h in range(HALVES)] for t in range(PACK)]
 
-        nc.vector.memset(kb_plane[:].rearrange("p z c -> p (z c)").bitcast(I32), 0)
+        def half(h):
+            return slice(h * BANK, (h + 1) * BANK)
+
+        def col(t):
+            return slice(t, t + 1)
+
+        nc.vector.memset(kb_plane[:].rearrange("p g c -> p (g c)").bitcast(I32), 0)
         nc.vector.memset(ident[:], 0.0)
-        nc.gpsimd.dma_start(out=cw_rows[:, :, :4], in_=cw1[0].rearrange("(h p c) -> p h c", h=HALVES, c=4))
-        make_identity(nc, ident[:], nomemset=True)
-        nc.gpsimd.memset(qa_plane_raw[:].bitcast(I32), 0)
-        nc.vector.memset(ka_plane[:].bitcast(I32), 0)
+        nc.gpsimd.memset(ka_plane[:].bitcast(I32), 0)
+        nc.vector.memset(qa_plane_raw[:].bitcast(I32), 0)
         nc.vector.memset(ones[:], 1.0)
-        nc.vector.memset(prods[:, :, 2], -1.0)
-        nc.vector.tensor_scalar(out=sums[:, :, 2], in0=ones[:], scalar1=0.1 / 0.7, scalar2=None, op0=ALU.mult)
+        nc.vector.memset(factors[:, :, 2], -1.0)
+        nc.vector.tensor_scalar(out=terms[:, :, 2], in0=ones[:], scalar1=FLOOR / SHARPNESS, scalar2=None, op0=ALU.mult)
+
+        def plane_rows(r):
+            return slice(r, P, QUADRANT)
+
+        def scale_rows(r):
+            return slice(r, SCALE_ROWS, 4)
 
         def load_qb(g):
-            nc.sync.dma_start(out=qb_raw[g][:], in_=qb[g * 512 : (g + 1) * 512, :].rearrange("(p j) c -> p j c", j=PACK))
-
-        def load_ka(h):
-            words = ka_words[0].rearrange("p n t -> p (n t)")
-            nc.sync.dma_start(out=ka_codes[h][:].bitcast(I32), in_=words[:, 4 * BANK * h : 4 * BANK * (h + 1)].bitcast(I32))
+            rows = qb[g * K_PASS : (g + 1) * K_PASS, :]
+            nc.sync.dma_start(out=qb_raw[g][:], in_=rows.rearrange("(p j) c -> p j c", j=PACK))
 
         def load_kb(g):
             nc.sync.dma_start(out=kb_codes[g][:].bitcast(I32), in_=kb_words[g].bitcast(I32))
 
+        for r in range(4):
+            nc.gpsimd.dma_start(out=ka_plane[plane_rows(r), :].bitcast(I32), in_=ka_scales[0, scale_rows(r), :].bitcast(I32))
+        make_identity(nc, ident[:], nomemset=True)
+
         load_qb(0)
-        for u in range(4):
+        for r in range(4):
             nc.sync.dma_start(
-                out=kb_plane[u:P:32, :, :].bitcast(I32),
-                in_=kb_scales[:, u:16:4, :].rearrange("z r c -> r z c").bitcast(I32),
-            )
-        for u in range(4):
-            nc.gpsimd.dma_start(
-                out=qa_plane_raw[u:P:32, :].bitcast(I32), in_=qa_scales[0, u:16:4, :].bitcast(I32)
+                out=kb_plane[plane_rows(r), :, :].bitcast(I32),
+                in_=kb_scales[:, scale_rows(r), :].rearrange("g r c -> r g c").bitcast(I32),
             )
         load_kb(0)
         nc.sync.dma_start(out=qa_raw[:].bitcast(I32), in_=qa_words[0].bitcast(I32))
         load_qb(1)
-        for u in range(4):
-            nc.sync.dma_start(
-                out=ka_plane[u:P:32, :].bitcast(I32), in_=ka_scales[0, u:16:4, :].bitcast(I32)
-            )
+        for r in range(4):
+            nc.sync.dma_start(out=qa_plane_raw[plane_rows(r), :].bitcast(I32), in_=qa_scales[0, scale_rows(r), :].bitcast(I32))
         load_kb(1)
-        load_ka(0)
-        load_ka(1)
+        ka_rows = ka_words[0].rearrange("p n j -> p (n j)").bitcast(I32)
+        for h in range(HALVES):
+            nc.sync.dma_start(out=ka_codes[h][:].bitcast(I32), in_=ka_rows[:, half(h)])
+        nc.sync.dma_start(out=cw_rows[:, :, :PACK], in_=cw1[0].rearrange("(h n c) -> n h c", h=HALVES, c=PACK))
+        nc.sync.dma_start(out=cw[:], in_=cw1[0].partition_broadcast(P))
 
         def round_qb(g):
             src = qb_raw[g][:].rearrange("p j (m t) -> p m t j", t=PACK)
             dst = qb_bf[g][:].rearrange("p t m j -> p m t j")
-            nc.vector.tensor_copy(out=dst[:, :M_VECTOR], in_=src[:, :M_VECTOR])
-            nc.scalar.activation(out=dst[:, M_VECTOR:], in_=src[:, M_VECTOR:], func=ACT.Copy)
+            nc.vector.tensor_copy(out=dst[:, :QB_GROUPS_VECTOR], in_=src[:, :QB_GROUPS_VECTOR])
+            nc.scalar.activation(out=dst[:, QB_GROUPS_VECTOR:], in_=src[:, QB_GROUPS_VECTOR:], func=ACT.Copy)
 
-        def quantize_qb(g, t0, t1):
+        def quantize_qb(g, t):
             nc.vector.quantize_mx(
-                out=qb_codes[g][:, t0 * P : t1 * P].bitcast(FP8X4),
-                scales=qb_plane[g][:, t0 * P : t1 * P],
-                in_=qb_bf[g][:, t0:t1].rearrange("p t m j -> p (t m j)"),
+                out=qb_codes[g][:, t * P : (t + 1) * P].bitcast(FP8X4),
+                scales=qb_plane[g][:, t * P : (t + 1) * P],
+                in_=qb_bf[g][:, t].rearrange("p m j -> p (m j)"),
             )
 
-        def product_b(g, t, h, start, stop):
+        def product_b(g, t, h):
             nc.tensor.matmul_mx(
                 out=acc[t][h][:],
                 lhsT=qb_codes[g][:, t * P : (t + 1) * P].bitcast(FP8X4),
                 lhsT_scale=qb_plane[g][:, t * P : (t + 1) * P],
                 rhs=kb_codes[g][:, 2 * BANK * h : 2 * BANK * (h + 1)].bitcast(FP4X4),
-                rhs_scale=kb_plane[:, g, BANK * h : BANK * (h + 1)],
-                start=start,
-                stop=stop,
+                rhs_scale=kb_plane[:, g, half(h)],
+                start=(g == 0),
+                stop=False,
             )
 
-        def product_a(t, h, stop):
+        def product_a(t, h):
             nc.tensor.matmul_mx(
                 out=acc[t][h][:],
                 lhsT=qa_codes[:, 2 * P * t : 2 * P * (t + 1)].bitcast(FP4X4),
                 lhsT_scale=qa_plane[:, t * P : (t + 1) * P],
                 rhs=ka_codes[h][:].bitcast(FP8X4),
-                rhs_scale=ka_plane[:, BANK * h : BANK * (h + 1)],
+                rhs_scale=ka_plane[:, half(h)],
                 start=False,
-                stop=stop,
+                stop=True,
             )
 
-        def spread_cw(banks, src):
-            for h in range(HALVES):
-                for c in range(4):
-                    nc.tensor.transpose(
-                        banks[h][:].rearrange("p (n c) -> p c n", c=4)[:, c],
-                        src[:, h, c : c + 1].to_broadcast([P, P]),
-                        ident[:],
-                    )
-
-        spread_cw(acc[3], cw_rows)
         round_qb(0)
         for t in range(PACK):
-            quantize_qb(0, t, t + 1)
-        for h in range(HALVES):
-            nc.scalar.activation(out=cw[:, h * BANK : (h + 1) * BANK], in_=acc[3][h][:], func=ACT.Copy, scale=256.0)
+            quantize_qb(0, t)
         for t in range(PACK):
             for h in range(HALVES):
-                product_b(0, t, h, True, False)
+                product_b(0, t, h)
         nc.vector.tensor_copy(
             out=qa_codes[:].rearrange("p (t m b) -> p t m b", t=PACK, b=2),
             in_=qa_raw[:].rearrange("p (m t b) -> p t m b", t=PACK, b=2),
         )
-        nc.vector.tensor_scalar(out=cw_cols[:], in0=cw_rows[:, :, :4], scalar1=256.0, scalar2=None, op0=ALU.mult)
         round_qb(1)
-        quantize_qb(1, 0, 1)
+        quantize_qb(1, 0)
         nc.vector.tensor_copy(
             out=qa_plane[:].rearrange("p (t m) -> p t m", t=PACK),
             in_=qa_plane_raw[:].rearrange("p (m t) -> p t m", t=PACK),
         )
         for t in range(1, PACK):
-            quantize_qb(1, t, t + 1)
+            quantize_qb(1, t)
         for t in range(PACK):
             for h in range(HALVES):
-                product_b(1, t, h, False, False)
+                product_b(1, t, h)
             for h in range(HALVES):
-                product_a(t, h, True)
+                product_a(t, h)
 
-        def half(h):
-            return slice(h * BANK, (h + 1) * BANK)
-
-        def sum_abs(t, h):
+        def sum_magnitudes(t, h):
             nc.scalar.activation(
-                out=e[t][:, half(h)], in_=acc[t][h][:], func=ACT.Abs, scale=1.0 / (0.7 * I), accum_out=sums[:, t, h : h + 1]
+                out=e[t][:, half(h)],
+                in_=acc[t][h][:],
+                func=ACT.Abs,
+                scale=1.0 / (SHARPNESS * I),
+                accum_out=terms[:, t, h : h + 1],
             )
 
-        def find_max(t, h):
+        def copy_and_max(t, h):
             nc.vector.tensor_scalar(
-                out=a[t][:, half(h)],
+                out=scores[t][:, half(h)],
                 in0=acc[t][h][:],
                 scalar1=1.0,
-                scalar2=None if h == 0 else first_max[:, t : t + 1],
+                scalar2=None if h == 0 else first_max[:, col(t)],
                 op0=ALU.mult,
                 op1=ALU.max,
-                accum_out=first_max[:, t : t + 1] if h == 0 else prods[:, t, 0:1],
+                accum_out=first_max[:, col(t)] if h == 0 else factors[:, t, 0:1],
             )
 
-        def make_denom(t):
-            nc.vector.tensor_reduce(out=denom[:, t : t + 1], in_=sums[:, t, 0:3], axis=AX.X, op=ALU.add)
+        def make_divisor(t):
+            nc.vector.tensor_reduce(out=divisor[:, col(t)], in_=terms[:, t, 0:3], axis=AX.X, op=ALU.add)
 
-        def make_sharp(t):
-            nc.vector.reciprocal(out=prods[:, t, 1:2], in_=denom[:, t : t + 1])
+        def invert_divisor(t):
+            nc.vector.reciprocal(out=factors[:, t, 1:2], in_=divisor[:, col(t)])
 
         def make_shift(t):
-            nc.vector.tensor_reduce(out=shift[:, t : t + 1], in_=prods[:, t, 0:3], axis=AX.X, op=ALU.mult)
+            nc.vector.tensor_reduce(out=shift[:, col(t)], in_=factors[:, t, 0:3], axis=AX.X, op=ALU.mult)
 
         def exponentiate(t):
             nc.scalar.activation(
                 out=e[t][:],
-                in_=a[t][:],
+                in_=scores[t][:],
                 func=ACT.Exp,
-                scale=prods[:, t, 1:2],
-                bias=shift[:, t : t + 1],
-                accum_out=exp_sum[:, t : t + 1],
+                scale=factors[:, t, 1:2],
+                bias=shift[:, col(t)],
+                accum_out=exp_sum[:, col(t)],
             )
 
         def make_norm(t):
-            nc.vector.reciprocal(out=norm[:, t : t + 1], in_=exp_sum[:, t : t + 1])
+            nc.vector.reciprocal(out=norm[:, col(t)], in_=exp_sum[:, col(t)])
 
-        def weigh(t, c0, c1):
-            h = c0 // BANK
+        def spread_weights():
+            nc.gpsimd.tensor_scalar(
+                out=cw_gained[:], in0=cw_rows[:, :, :PACK], scalar1=GAIN, scalar2=0.0, op0=ALU.mult, op1=ALU.add
+            )
+            for h in range(HALVES):
+                for c in range(PACK):
+                    nc.tensor.transpose(
+                        acc[0][h][:].rearrange("p (n c) -> p c n", c=PACK)[:, c],
+                        cw_gained[:, h, c : c + 1].to_broadcast([P, P]),
+                        ident[:],
+                    )
+
+        def weigh(t, h, cols):
             nc.vector.scalar_tensor_tensor(
-                out=y[:, t, c0:c1],
-                in0=e[t][:, c0:c1],
-                scalar=norm[:, t : t + 1],
-                in1=acc[0][h][:, c0 - h * BANK : c1 - h * BANK],
+                out=y[:, h, t, cols],
+                in0=e[t][:, half(h)][:, cols],
+                scalar=norm[:, col(t)],
+                in1=acc[0][h][:, cols],
                 op0=ALU.mult,
                 op1=ALU.mult,
             )
 
-        def weigh_first(u, t, c0):
-            nc.gpsimd.tensor_tensor(out=u[:], in0=e[t][:, c0:], in1=cw[:, c0:], op=ALU.mult)
+        def gpsimd_times_weights(e_cw, t, cols):
+            nc.gpsimd.tensor_tensor(out=e_cw, in0=e[t][:, cols], in1=cw[:, cols], op=ALU.mult)
 
-        def weigh_second(u, t, c0):
-            nc.gpsimd.tensor_scalar(out=y[:, t, c0:], in0=u[:], scalar1=norm[:, t : t + 1], scalar2=0.0, op0=ALU.mult, op1=ALU.add)
-
-        out_rows = out_0.rearrange("(p t) c -> p t c", t=PACK)
-
-        def store_y(t, c0, c1):
-            nc.sync.dma_start(out=out_rows[:, t, c0:c1], in_=y[:, t, c0:c1])
-
-        def round_y(c0, c1, on_scalar):
-            src = y[:, :, c0:c1].rearrange("p t (c i) -> p c t i", i=4)
-            dst = y_bf[:, c0:c1, :].rearrange("p (c i) t -> p c t i", i=4)
-            if on_scalar:
-                nc.scalar.activation(out=dst, in_=src, func=ACT.Copy)
-            else:
-                nc.vector.tensor_copy(out=dst, in_=src)
-
-        def quantize_y(c0, c1):
-            nc.vector.quantize_mx(
-                out=y_codes[:, c0:c1].bitcast(FP8X4), scales=y_plane[:, c0:c1], in_=y_bf[:, c0:c1, :].rearrange("p c t -> p (c t)")
+        def gpsimd_normalise(e_cw, t, h):
+            nc.gpsimd.tensor_scalar(
+                out=y[:, h, t, :], in0=e_cw, scalar1=norm[:, col(t)], scalar2=GAIN, op0=ALU.mult, op1=ALU.mult
             )
 
-        code_rows = out_1[0].rearrange("p n t -> p (n t)").bitcast(I32)
+        out_rows = out_0.rearrange("(p t) (h c) -> p t h c", t=PACK, h=HALVES)
 
-        def store_codes(c0, c1):
-            nc.sync.dma_start(out=code_rows[:, c0:c1], in_=y_codes[:, c0:c1].bitcast(I32))
+        def store_y(t, h0, h1):
+            nc.sync.dma_start(out=out_rows[:, t, h0:h1, :], in_=y[:, h0:h1, t, :])
 
-        sum_abs(0, 0)
-        find_max(0, 0)
-        sum_abs(0, 1)
-        make_denom(0)
-        find_max(0, 1)
-        make_sharp(0)
-        spread_cw(acc[0], cw_cols)
-        sum_abs(1, 0)
-        sum_abs(1, 1)
-        sum_abs(2, 0)
-        find_max(1, 0)
+        def round_views(c0, c1):
+            h = c0 // BANK
+            src = y[:, h, :, c0 - h * BANK : c1 - h * BANK].rearrange("p t (c i) -> p c t i", i=4)
+            dst = y_bf[:, c0:c1, :].rearrange("p (c i) t -> p c t i", i=4)
+            return dst, src
+
+        def round_y_scalar(c0, c1):
+            dst, src = round_views(c0, c1)
+            nc.scalar.activation(out=dst, in_=src, func=ACT.Copy)
+
+        def round_y_vector(c0, c1):
+            dst, src = round_views(c0, c1)
+            nc.vector.tensor_copy(out=dst, in_=src)
+
+        def quantize_y(n):
+            cols = slice(n * QUARTER, (n + 1) * QUARTER)
+            nc.vector.quantize_mx(
+                out=y_codes[:, cols].bitcast(FP8X4), scales=y_plane[:, cols], in_=y_bf[:, cols, :].rearrange("p c t -> p (c t)")
+            )
+
+        code_rows = out_1[0].rearrange("p n j -> p (n j)").bitcast(I32)
+
+        def store_codes(n0, n1):
+            cols = slice(n0 * QUARTER, n1 * QUARTER)
+            nc.sync.dma_start(out=code_rows[:, cols], in_=y_codes[:, cols].bitcast(I32))
+
+        whole = slice(0, BANK)
+
+        sum_magnitudes(0, 0)
+        copy_and_max(0, 0)
+        sum_magnitudes(0, 1)
+        make_divisor(0)
+        copy_and_max(0, 1)
+        invert_divisor(0)
+        spread_weights()
+        sum_magnitudes(1, 0)
+        sum_magnitudes(1, 1)
+        sum_magnitudes(2, 0)
         make_shift(0)
+        copy_and_max(1, 0)
         exponentiate(0)
-        make_denom(1)
-        find_max(1, 1)
-        make_sharp(1)
-        weigh_first(u0, 0, 0)
-        sum_abs(2, 1)
-        sum_abs(3, 0)
-        sum_abs(3, 1)
-        find_max(2, 0)
+        make_divisor(1)
+        copy_and_max(1, 1)
+        invert_divisor(1)
+        gpsimd_times_weights(e_cw0[:], 0, slice(0, I))
+        sum_magnitudes(2, 1)
+        sum_magnitudes(3, 0)
+        sum_magnitudes(3, 1)
+        copy_and_max(2, 0)
         make_shift(1)
         exponentiate(1)
         make_norm(0)
-        weigh_second(u0, 0, 0)
-        store_y(0, 0, I)
-        make_denom(2)
-        find_max(2, 1)
-        make_sharp(2)
-        find_max(3, 0)
+        for h in range(HALVES):
+            gpsimd_normalise(e_cw0[:, half(h)], 0, h)
+            store_y(0, h, h + 1)
+        make_divisor(2)
+        copy_and_max(2, 1)
+        invert_divisor(2)
+        copy_and_max(3, 0)
         make_shift(2)
         exponentiate(2)
-        make_denom(3)
-        find_max(3, 1)
-        make_sharp(3)
+        make_divisor(3)
+        copy_and_max(3, 1)
+        invert_divisor(3)
         make_norm(1)
-        weigh_first(u1, 1, BANK)
-        weigh_second(u1, 1, BANK)
         make_shift(3)
         exponentiate(3)
-        weigh(1, 0, BANK)
+
+        weigh(1, 0, whole)
+        gpsimd_times_weights(e_cw2[:], 2, half(1))
         make_norm(2)
-        weigh(2, 0, BANK)
-        weigh(2, BANK, I)
-        store_y(2, 0, I)
-        store_y(1, 0, I)
+        gpsimd_normalise(e_cw2[:], 2, 1)
+        weigh(1, 1, whole)
+        store_y(1, 0, HALVES)
+        weigh(2, 0, whole)
+        store_y(2, 0, 1)
+        store_y(2, 1, 2)
         make_norm(3)
 
-        weigh(3, 0, 256)
-        round_y(0, 256, True)
-        weigh(3, 256, 512)
-        store_y(3, 0, BANK)
-        weigh(3, 512, 1024)
-        store_y(3, BANK, I)
-        round_y(256, 512, False)
-        round_y(512, 768, True)
-        quantize_y(0, 256)
-        round_y(832, 1024, False)
-        quantize_y(256, 512)
-        store_codes(0, BANK)
-        round_y(768, 832, True)
-        quantize_y(512, 768)
-        store_codes(BANK, 768)
-        quantize_y(768, 1024)
-        store_codes(768, I)
-        for u in range(4):
-            queue = nc.scalar if u % 2 == 0 else nc.sync
-            queue.dma_start(out=out_2[0, u:16:4, :].bitcast(I32), in_=y_plane[u:P:32, :].bitcast(I32))
+        split = 3 * QUARTER + LAST_COLS_SCALAR
+        weigh(3, 0, slice(0, QUARTER))
+        round_y_scalar(0, QUARTER)
+        weigh(3, 0, slice(QUARTER, BANK))
+        weigh(3, 1, whole)
+        store_y(3, 0, HALVES)
+        round_y_vector(QUARTER, 2 * QUARTER)
+        round_y_scalar(2 * QUARTER, 3 * QUARTER)
+        quantize_y(0)
+        round_y_vector(split, I)
+        quantize_y(1)
+        store_codes(0, 2)
+        round_y_scalar(3 * QUARTER, split)
+        quantize_y(2)
+        store_codes(2, 3)
+        quantize_y(3)
+        store_codes(3, 4)
+        for r in range(4):
+            queue = nc.scalar if r % 2 == 0 else nc.sync
+            queue.dma_start(out=out_2[0, scale_rows(r), :].bitcast(I32), in_=y_plane[plane_rows(r), :].bitcast(I32))

from contextlib import ExitStack

import concourse.mybir as mybir
from concourse.masks import make_identity

K, L, Q, I = 512, 1024, 512, 1024
FLOPS = 2 * (K + L) * Q * I

F32 = mybir.dt.float32
BF16 = mybir.dt.bfloat16
I32 = mybir.dt.int32
U32 = mybir.dt.uint32
U8 = mybir.dt.uint8
FP8X4 = mybir.dt.float8_e4m3fn_x4
FP4X4 = mybir.dt.float4_e2m1fn_x4
ALU = mybir.AluOpType
ACT = mybir.ActivationFunctionType
AX = mybir.AxisListType

P = 128
PACK = 4
K_PASS = P * PACK
B_PASSES = L // K_PASS
BANK = 512
HALVES = I // BANK
QUADRANT = 32
SCALE_ROWS = 16
QUARTER = I // 4
SHARPNESS = 0.7
FLOOR = 0.1
GAIN = 256.0
QB_GROUPS_VECTOR = 84
LAST_COLS_SCALAR = 64


def tile_mix_shares_by_row_scale_pl_kernel(
    tc, qa_words, qa_scales, ka_words, ka_scales, qb, kb_words, kb_scales, cw1, out_0, out_1, out_2
):
    nc = tc.nc
    with ExitStack() as ctx:
        keep = ctx.enter_context(tc.tile_pool(name="keep", bufs=1))
        psum = ctx.enter_context(tc.psum_pool(name="psum", bufs=1))
        ctx.enter_context(tc.manual_schedule())

        qb_raw = [keep.tile([P, PACK, Q], F32, name="qb_raw%d" % g) for g in range(B_PASSES)]
        qb_bf = [keep.tile([P, PACK, P, PACK], BF16, name="qb_bf%d" % g, align_bytes=64) for g in range(B_PASSES)]
        qb_codes = [keep.tile([P, Q], U32, name="qb_codes%d" % g, align_bytes=64) for g in range(B_PASSES)]
        qb_plane = [keep.tile([P, Q], U8, name="qb_plane%d" % g, align_bytes=64) for g in range(B_PASSES)]
        qa_raw = keep.tile([P, 2 * Q], U8, align_bytes=64)
        qa_codes = keep.tile([P, 2 * Q], U8, align_bytes=64)
        qa_plane_raw = keep.tile([P, Q], U8, align_bytes=64)
        qa_plane = keep.tile([P, Q], U8, align_bytes=64)
        ka_codes = [keep.tile([P, BANK], U32, name="ka_codes%d" % h, align_bytes=64) for h in range(HALVES)]
        ka_plane = keep.tile([P, I], U8, align_bytes=64)
        kb_codes = [keep.tile([P, 2 * I], U8, name="kb_codes%d" % g, align_bytes=64) for g in range(B_PASSES)]
        kb_plane = keep.tile([P, B_PASSES, I], U8, align_bytes=64)
        cw = keep.tile([P, I], F32)
        scores = [keep.tile([P, I], F32, name="scores%d" % t) for t in range(PACK)]
        e = [keep.tile([P, I], F32, name="e%d" % t) for t in range(PACK)]
        y = keep.tile([P, HALVES, PACK, BANK], F32)
        y_bf = keep.tile([P, I, PACK], BF16, align_bytes=64)
        y_codes = keep.tile([P, I], U32, align_bytes=64)
        y_plane = keep.tile([P, I], U8, align_bytes=64)
        terms = keep.tile([P, PACK, 4], F32)
        factors = keep.tile([P, PACK, 4], F32)
        ones = keep.tile([P, PACK], F32)
        first_max = keep.tile([P, PACK], F32)
        exp_sum = keep.tile([P, PACK], F32)
        divisor = keep.tile([P, PACK], F32)
        shift = keep.tile([P, PACK], F32)
        norm = keep.tile([P, PACK], F32)
        cw_rows = keep.tile([P, HALVES, 8], F32)
        cw_gained = keep.tile([P, HALVES, PACK], F32)
        ident = keep.tile([P, P], F32)
        e_cw0 = keep.tile([P, I], F32)
        e_cw2 = keep.tile([P, BANK], F32)
        acc = [[psum.tile([P, BANK], F32, name="acc%d_%d" % (t, h)) for h in range(HALVES)] for t in range(PACK)]

        def half(h):
            return slice(h * BANK, (h + 1) * BANK)

        def col(t):
            return slice(t, t + 1)

        nc.vector.memset(kb_plane[:].rearrange("p g c -> p (g c)").bitcast(I32), 0)
        nc.vector.memset(ident[:], 0.0)
        nc.gpsimd.memset(ka_plane[:].bitcast(I32), 0)
        nc.vector.memset(qa_plane_raw[:].bitcast(I32), 0)
        nc.vector.memset(ones[:], 1.0)
        nc.vector.memset(factors[:, :, 2], -1.0)
        nc.vector.tensor_scalar(out=terms[:, :, 2], in0=ones[:], scalar1=FLOOR / SHARPNESS, scalar2=None, op0=ALU.mult)

        def plane_rows(r):
            return slice(r, P, QUADRANT)

        def scale_rows(r):
            return slice(r, SCALE_ROWS, 4)

        def load_qb(g):
            rows = qb[g * K_PASS : (g + 1) * K_PASS, :]
            nc.sync.dma_start(out=qb_raw[g][:], in_=rows.rearrange("(p j) c -> p j c", j=PACK))

        def load_kb(g):
            nc.sync.dma_start(out=kb_codes[g][:].bitcast(I32), in_=kb_words[g].bitcast(I32))

        for r in range(4):
            nc.gpsimd.dma_start(out=ka_plane[plane_rows(r), :].bitcast(I32), in_=ka_scales[0, scale_rows(r), :].bitcast(I32))
        make_identity(nc, ident[:], nomemset=True)

        load_qb(0)
        for r in range(4):
            nc.sync.dma_start(
                out=kb_plane[plane_rows(r), :, :].bitcast(I32),
                in_=kb_scales[:, scale_rows(r), :].rearrange("g r c -> r g c").bitcast(I32),
            )
        load_kb(0)
        nc.sync.dma_start(out=qa_raw[:].bitcast(I32), in_=qa_words[0].bitcast(I32))
        load_qb(1)
        for r in range(4):
            nc.sync.dma_start(out=qa_plane_raw[plane_rows(r), :].bitcast(I32), in_=qa_scales[0, scale_rows(r), :].bitcast(I32))
        load_kb(1)
        ka_rows = ka_words[0].rearrange("p n j -> p (n j)").bitcast(I32)
        for h in range(HALVES):
            nc.sync.dma_start(out=ka_codes[h][:].bitcast(I32), in_=ka_rows[:, half(h)])
        nc.sync.dma_start(out=cw_rows[:, :, :PACK], in_=cw1[0].rearrange("(h n c) -> n h c", h=HALVES, c=PACK))
        nc.sync.dma_start(out=cw[:], in_=cw1[0].partition_broadcast(P))

        def round_qb(g):
            src = qb_raw[g][:].rearrange("p j (m t) -> p m t j", t=PACK)
            dst = qb_bf[g][:].rearrange("p t m j -> p m t j")
            nc.vector.tensor_copy(out=dst[:, :QB_GROUPS_VECTOR], in_=src[:, :QB_GROUPS_VECTOR])
            nc.scalar.activation(out=dst[:, QB_GROUPS_VECTOR:], in_=src[:, QB_GROUPS_VECTOR:], func=ACT.Copy)

        def quantize_qb(g, t):
            nc.vector.quantize_mx(
                out=qb_codes[g][:, t * P : (t + 1) * P].bitcast(FP8X4),
                scales=qb_plane[g][:, t * P : (t + 1) * P],
                in_=qb_bf[g][:, t].rearrange("p m j -> p (m j)"),
            )

        def product_b(g, t, h):
            nc.tensor.matmul_mx(
                out=acc[t][h][:],
                lhsT=qb_codes[g][:, t * P : (t + 1) * P].bitcast(FP8X4),
                lhsT_scale=qb_plane[g][:, t * P : (t + 1) * P],
                rhs=kb_codes[g][:, 2 * BANK * h : 2 * BANK * (h + 1)].bitcast(FP4X4),
                rhs_scale=kb_plane[:, g, half(h)],
                start=(g == 0),
                stop=False,
            )

        def product_a(t, h):
            nc.tensor.matmul_mx(
                out=acc[t][h][:],
                lhsT=qa_codes[:, 2 * P * t : 2 * P * (t + 1)].bitcast(FP4X4),
                lhsT_scale=qa_plane[:, t * P : (t + 1) * P],
                rhs=ka_codes[h][:].bitcast(FP8X4),
                rhs_scale=ka_plane[:, half(h)],
                start=False,
                stop=True,
            )

        round_qb(0)
        for t in range(PACK):
            quantize_qb(0, t)
        for t in range(PACK):
            for h in range(HALVES):
                product_b(0, t, h)
        nc.vector.tensor_copy(
            out=qa_codes[:].rearrange("p (t m b) -> p t m b", t=PACK, b=2),
            in_=qa_raw[:].rearrange("p (m t b) -> p t m b", t=PACK, b=2),
        )
        round_qb(1)
        quantize_qb(1, 0)
        nc.vector.tensor_copy(
            out=qa_plane[:].rearrange("p (t m) -> p t m", t=PACK),
            in_=qa_plane_raw[:].rearrange("p (m t) -> p t m", t=PACK),
        )
        for t in range(1, PACK):
            quantize_qb(1, t)
        for t in range(PACK):
            for h in range(HALVES):
                product_b(1, t, h)
            for h in range(HALVES):
                product_a(t, h)

        def sum_magnitudes(t, h):
            nc.scalar.activation(
                out=e[t][:, half(h)],
                in_=acc[t][h][:],
                func=ACT.Abs,
                scale=1.0 / (SHARPNESS * I),
                accum_out=terms[:, t, h : h + 1],
            )

        def copy_and_max(t, h):
            nc.vector.tensor_scalar(
                out=scores[t][:, half(h)],
                in0=acc[t][h][:],
                scalar1=1.0,
                scalar2=None if h == 0 else first_max[:, col(t)],
                op0=ALU.mult,
                op1=ALU.max,
                accum_out=first_max[:, col(t)] if h == 0 else factors[:, t, 0:1],
            )

        def make_divisor(t):
            nc.vector.tensor_reduce(out=divisor[:, col(t)], in_=terms[:, t, 0:3], axis=AX.X, op=ALU.add)

        def invert_divisor(t):
            nc.vector.reciprocal(out=factors[:, t, 1:2], in_=divisor[:, col(t)])

        def make_shift(t):
            nc.vector.tensor_reduce(out=shift[:, col(t)], in_=factors[:, t, 0:3], axis=AX.X, op=ALU.mult)

        def exponentiate(t):
            nc.scalar.activation(
                out=e[t][:],
                in_=scores[t][:],
                func=ACT.Exp,
                scale=factors[:, t, 1:2],
                bias=shift[:, col(t)],
                accum_out=exp_sum[:, col(t)],
            )

        def make_norm(t):
            nc.vector.reciprocal(out=norm[:, col(t)], in_=exp_sum[:, col(t)])

        def spread_weights():
            nc.gpsimd.tensor_scalar(
                out=cw_gained[:], in0=cw_rows[:, :, :PACK], scalar1=GAIN, scalar2=0.0, op0=ALU.mult, op1=ALU.add
            )
            for h in range(HALVES):
                for c in range(PACK):
                    nc.tensor.transpose(
                        acc[0][h][:].rearrange("p (n c) -> p c n", c=PACK)[:, c],
                        cw_gained[:, h, c : c + 1].to_broadcast([P, P]),
                        ident[:],
                    )

        def weigh(t, h, cols):
            nc.vector.scalar_tensor_tensor(
                out=y[:, h, t, cols],
                in0=e[t][:, half(h)][:, cols],
                scalar=norm[:, col(t)],
                in1=acc[0][h][:, cols],
                op0=ALU.mult,
                op1=ALU.mult,
            )

        def gpsimd_times_weights(e_cw, t, cols):
            nc.gpsimd.tensor_tensor(out=e_cw, in0=e[t][:, cols], in1=cw[:, cols], op=ALU.mult)

        def gpsimd_normalise(e_cw, t, h):
            nc.gpsimd.tensor_scalar(
                out=y[:, h, t, :], in0=e_cw, scalar1=norm[:, col(t)], scalar2=GAIN, op0=ALU.mult, op1=ALU.mult
            )

        out_rows = out_0.rearrange("(p t) (h c) -> p t h c", t=PACK, h=HALVES)

        def store_y(t, h0, h1):
            nc.sync.dma_start(out=out_rows[:, t, h0:h1, :], in_=y[:, h0:h1, t, :])

        def round_views(c0, c1):
            h = c0 // BANK
            src = y[:, h, :, c0 - h * BANK : c1 - h * BANK].rearrange("p t (c i) -> p c t i", i=4)
            dst = y_bf[:, c0:c1, :].rearrange("p (c i) t -> p c t i", i=4)
            return dst, src

        def round_y_scalar(c0, c1):
            dst, src = round_views(c0, c1)
            nc.scalar.activation(out=dst, in_=src, func=ACT.Copy)

        def round_y_vector(c0, c1):
            dst, src = round_views(c0, c1)
            nc.vector.tensor_copy(out=dst, in_=src)

        def quantize_y(n):
            cols = slice(n * QUARTER, (n + 1) * QUARTER)
            nc.vector.quantize_mx(
                out=y_codes[:, cols].bitcast(FP8X4), scales=y_plane[:, cols], in_=y_bf[:, cols, :].rearrange("p c t -> p (c t)")
            )

        code_rows = out_1[0].rearrange("p n j -> p (n j)").bitcast(I32)

        def store_codes(n0, n1):
            cols = slice(n0 * QUARTER, n1 * QUARTER)
            nc.sync.dma_start(out=code_rows[:, cols], in_=y_codes[:, cols].bitcast(I32))

        whole = slice(0, BANK)

        sum_magnitudes(0, 0)
        copy_and_max(0, 0)
        sum_magnitudes(0, 1)
        make_divisor(0)
        copy_and_max(0, 1)
        invert_divisor(0)
        spread_weights()
        sum_magnitudes(1, 0)
        sum_magnitudes(1, 1)
        sum_magnitudes(2, 0)
        make_shift(0)
        copy_and_max(1, 0)
        exponentiate(0)
        make_divisor(1)
        copy_and_max(1, 1)
        invert_divisor(1)
        gpsimd_times_weights(e_cw0[:], 0, slice(0, I))
        sum_magnitudes(2, 1)
        sum_magnitudes(3, 0)
        sum_magnitudes(3, 1)
        copy_and_max(2, 0)
        make_shift(1)
        exponentiate(1)
        make_norm(0)
        for h in range(HALVES):
            gpsimd_normalise(e_cw0[:, half(h)], 0, h)
            store_y(0, h, h + 1)
        make_divisor(2)
        copy_and_max(2, 1)
        invert_divisor(2)
        copy_and_max(3, 0)
        make_shift(2)
        exponentiate(2)
        make_divisor(3)
        copy_and_max(3, 1)
        invert_divisor(3)
        make_norm(1)
        make_shift(3)
        exponentiate(3)

        weigh(1, 0, whole)
        gpsimd_times_weights(e_cw2[:], 2, half(1))
        make_norm(2)
        gpsimd_normalise(e_cw2[:], 2, 1)
        weigh(1, 1, whole)
        store_y(1, 0, HALVES)
        weigh(2, 0, whole)
        store_y(2, 0, 1)
        store_y(2, 1, 2)
        make_norm(3)

        split = 3 * QUARTER + LAST_COLS_SCALAR
        weigh(3, 0, slice(0, QUARTER))
        round_y_scalar(0, QUARTER)
        weigh(3, 0, slice(QUARTER, BANK))
        weigh(3, 1, whole)
        store_y(3, 0, HALVES)
        round_y_vector(QUARTER, 2 * QUARTER)
        round_y_scalar(2 * QUARTER, 3 * QUARTER)
        quantize_y(0)
        round_y_vector(split, I)
        quantize_y(1)
        store_codes(0, 2)
        round_y_scalar(3 * QUARTER, split)
        quantize_y(2)
        store_codes(2, 3)
        quantize_y(3)
        store_codes(3, 4)
        for r in range(4):
            queue = nc.scalar if r % 2 == 0 else nc.sync
            queue.dma_start(out=out_2[0, scale_rows(r), :].bitcast(I32), in_=y_plane[plane_rows(r), :].bitcast(I32))
